import numpy as np
import ml_dtypes


def mxq(x, axis, fmt="e4m3"):
    dtype, down = {"e4m3": (ml_dtypes.float8_e4m3fn, 7), "e5m2": (ml_dtypes.float8_e5m2, 14)}[fmt]
    v = np.moveaxis(np.asarray(x, np.float32).astype(ml_dtypes.bfloat16).astype(np.float64), axis, -1)
    blocks = v.reshape(v.shape[:-1] + (-1, 32))
    amax = np.abs(blocks).max(-1, keepdims=True)
    byte = np.maximum(np.where(amax > 0, np.frexp(amax)[1] - 1 + 127, 0) - down, 1)
    scale = np.exp2(byte - 127.0)
    codes = (blocks / scale).astype(np.float32).astype(dtype).astype(np.float64)
    return np.moveaxis((codes * scale).reshape(v.shape), -1, axis)


WIDE = False


def mx_kscale(k):
    if not WIDE:
        return np.ones(k)
    levels = np.array([10, -10, 5, -5, 0])
    if k % 512:
        return np.exp2(np.random.permutation(np.resize(levels, k // 32))).repeat(32)
    a = np.empty((k // 512, 16))
    for p in range(k // 512):
        a[p, :8] = np.random.permutation(np.resize(levels, 8))
        for g in range(8):
            far = levels[np.abs(levels - a[p, g]) >= 10]
            a[p, g + 8] = far[np.random.randint(len(far))]
    return np.exp2(a.ravel()).repeat(32)


def f64(x):
    return np.asarray(x).astype(np.float64)


def striped8(idx):
    return np.concatenate([v.reshape(-1, 16).T for v in idx]).astype(np.uint16)


def unstriped8(offs):
    return np.stack([offs[16 * g:16 * g + 16].T.reshape(-1) for g in range(8)]).astype(np.int64)


def split(x):
    m, e = np.frexp(f64(x))
    hi = np.ldexp(np.trunc(16.0 * m) / 16.0, e)
    return hi, f64(x) - hi


def silu(v):
    return v / (1.0 + np.exp(-np.maximum(v, -700.0)))


K, M, T, S = 512, 512, 2048, 512


def setup_inputs():
    n = np.random.standard_normal
    s = mx_kscale(K)[:, None]
    return {
        "xT": (n((K, T)) * s).astype(np.float32),
        "w": (n((K, M)) / np.sqrt(K) / s).astype(np.float32),
        "wgt": np.repeat(np.random.uniform(0.5, 2.0, (8, S)), 16, axis=0).astype(np.float32),
        "b": (0.3 * n(512)).astype(np.float32),
        "offs": striped8(np.stack([np.random.permutation(T)[:S] for _ in range(8)])),
    }


def reference(xT, w, wgt, b, offs):
    idx = unstriped8(offs)
    group = np.arange(K) % 512 // 64
    xg = f64(wgt)[np.arange(K) // 4 % 128] * f64(xT)[np.arange(K)[:, None], idx[group]]
    xT_ = mxq(xg, 0, "e4m3")
    w_hi, w_lo = split(w)
    w_hi_, w_lo_ = mxq(w_hi, 0, "e4m3"), mxq(w_lo, 0, "e4m3")
    y = xT_.T @ w_hi_ + xT_.T @ w_lo_
    return silu(y + f64(b)[None, :])

@@ -1,0 +1,194 @@
+from contextlib import ExitStack
+
+import concourse.mybir as mybir
+
+K, M, T, S = 512, 512, 2048, 512
+P = 128
+PACK = 4
+TOK = 128
+HALF = 256
+WARM = 12
+FLOPS = 2 * 2 * K * M * S
+
+F32 = mybir.dt.float32
+BF16 = mybir.dt.bfloat16
+I32 = mybir.dt.int32
+U32 = mybir.dt.uint32
+U16 = mybir.dt.uint16
+U8 = mybir.dt.uint8
+FP8X4 = mybir.dt.float8_e4m3fn_x4
+ALU = mybir.AluOpType
+ACT = mybir.ActivationFunctionType
+
+HI_MASK = -(1 << 20)
+
+
+def tile_list_heads_tm_hl_silu_kernel(tc, xT, w, wgt, b, offs, out):
+    nc = tc.nc
+    with ExitStack() as ctx:
+        keep = ctx.enter_context(tc.tile_pool(name="keep", bufs=1))
+        psum = ctx.enter_context(tc.psum_pool(name="psum", bufs=1))
+
+        wgt_rows = keep.tile([P, P], F32, name="wgt_rows")
+        nc.sync.dma_start(
+            out=wgt_rows[:],
+            in_=wgt.rearrange("(g r) (c m) -> g r c m", r=16, m=P)[:, 0:4, :, :].rearrange("g a c m -> g (a c) m"),
+        )
+        b_rows = keep.tile([P, P], F32, name="b_rows")
+        nc.sync.dma_start(
+            out=b_rows[:], in_=b.rearrange("(c m) -> c m", m=P).unsqueeze(0).to_broadcast([P // 4, 4, P])
+        )
+        offsets = keep.tile([P, S // 16], U16, name="offsets")
+        nc.sync.dma_start(offsets[:], offs)
+
+        w_f = keep.tile([P, PACK, M], F32, name="w_f", align_bytes=64)
+        w_view = w.rearrange("(p i) n -> p i n", i=PACK)
+        for h in range(2):
+            nc.sync.dma_start(out=w_f[:, 2 * h : 2 * h + 2, :], in_=w_view[:, 2 * h : 2 * h + 2, :])
+        x_view = xT.rearrange("(p i) t -> i p t", i=PACK)
+        planes = []
+        for i in range(PACK):
+            plane = keep.tile([P, T], F32, name=f"plane{i}")
+            nc.sync.dma_start(out=plane[:], in_=x_view[i])
+            planes.append(plane)
+
+        warm = keep.tile([P, 1], F32, name="warm")
+        nc.vector.memset(warm[:], 0.0)
+        nc.scalar.activation(warm[:], warm[:], ACT.Silu)
+
+
+        ones = keep.tile([P, P], F32, name="ones")
+        nc.vector.memset(ones[:], 1.0)
+        col = keep.tile([P, P], F32, name="col", align_bytes=64)
+        nc.vector.tensor_tensor_scan(col[:], ones[:], ones[:], 0.0, ALU.mult, ALU.add)
+        blocks = keep.tile([P, P], F32, name="blocks")
+        nc.vector.memset(blocks[:], 0.0)
+        for q in range(4):
+            nc.vector.memset(blocks[32 * q : 32 * q + 32, 32 * q : 32 * q + 32], 1.0)
+        row = keep.tile([P, P], F32, name="row", align_bytes=64)
+        nc.vector.transpose(row[:], col[:])
+        same = keep.tile([P, P], F32, name="same")
+        nc.vector.tensor_tensor(same[:], col[:], row[:], ALU.is_equal)
+        ident = keep.tile([P, P], F32, name="ident")
+        nc.vector.tensor_tensor(ident[:], same[:], blocks[:], ALU.mult)
+
+        wgt_cols = psum.tile([P, P], F32, name="wgt_cols")
+        nc.tensor.transpose(wgt_cols[:], wgt_rows[:], ident[:])
+        b_colp = psum.tile([P, P], F32, name="b_colp")
+        nc.tensor.transpose(b_colp[:], b_rows[:], ident[:])
+        wgt_rep = keep.tile([P, 4, P], F32, name="wgt_rep")
+        nc.scalar.copy(
+            wgt_rep[:].rearrange("p c (g r) -> p c g r", r=16),
+            wgt_cols[:].rearrange("m (g a c) -> m c g a", g=8, c=4)[:, :, :, 0:1].to_broadcast([P, 4, 8, 16]),
+        )
+        b_col = keep.tile([P, PACK], F32, name="b_col")
+        nc.scalar.copy(b_col[:], b_colp[:, 0:PACK])
+        wgt_allp = psum.tile([P, S], F32, name="wgt_allp")
+        b_allp = psum.tile([P, M], F32, name="b_allp")
+        for c in range(4):
+            nc.tensor.transpose(wgt_allp[:, c * P : (c + 1) * P], wgt_rep[:, c, :], ident[:])
+        for c in range(PACK):
+            nc.tensor.transpose(b_allp[:, c * P : (c + 1) * P], b_col[:, c : c + 1].to_broadcast([P, P]), ident[:])
+        wgt_t = keep.tile([P, S], F32, name="wgt_t")
+        nc.scalar.copy(wgt_t[:], wgt_allp[:])
+        b_all = keep.tile([P, M], F32, name="b_all")
+        nc.scalar.copy(b_all[:], b_allp[:])
+
+        hi_bits = keep.tile([P, PACK, M], I32, name="hi_bits")
+        lo_f = keep.tile([P, PACK, M], F32, name="lo_f")
+        hi_f = hi_bits[:].rearrange("p i n -> p (i n)").bitcast(F32).rearrange("p (i n) -> p i n", i=PACK)
+        w_bits = w_f[:].rearrange("p i n -> p (i n)").bitcast(I32).rearrange("p (i n) -> p i n", i=PACK)
+        for h in range(2):
+            r = slice(2 * h, 2 * h + 2)
+            nc.vector.tensor_scalar(hi_bits[:, r, :], w_bits[:, r, :], HI_MASK, None, ALU.bitwise_and)
+            nc.vector.tensor_tensor(lo_f[:, r, :], w_f[:, r, :], hi_f[:, r, :], ALU.subtract)
+        codes, scales = [], []
+        for name, part in (("hi", hi_f), ("lo", lo_f[:])):
+            grouped = keep.tile([P, M, PACK], BF16, name=f"grouped_{name}", align_bytes=64)
+            nc.scalar.copy(grouped[:], part.rearrange("p i n -> p n i"))
+            code = keep.tile([P, M], U32, name=f"codes_{name}", align_bytes=64)
+            scale = keep.tile([P, M], U8, name=f"scales_{name}", align_bytes=64)
+            nc.vector.quantize_mx(
+                out=code[:].bitcast(FP8X4), scales=scale[:], in_=grouped[:].rearrange("p n i -> p (n i)")
+            )
+            codes.append(code)
+            scales.append(scale)
+
+        g = keep.tile([P, PACK, S], F32, name="g", align_bytes=64)
+        xg = keep.tile([P, S, PACK], BF16, name="xg", align_bytes=64)
+        xc = keep.tile([P, S], U32, name="xc", align_bytes=64)
+        xs = keep.tile([P, S], U8, name="xs", align_bytes=64)
+
+        def gather(i, j0, n):
+            nc.vector.tensor_tensor(
+                g[:, i, j0 : j0 + n],
+                planes[i][:].indirect(offsets[:, j0 // 16 : (j0 + n) // 16]),
+                wgt_t[:, j0 : j0 + n],
+                ALU.mult,
+            )
+
+        def interleave(i0, j0, n):
+            nc.scalar.copy(
+                xg[:, j0 : j0 + n, i0 : i0 + 2],
+                g[:, i0 : i0 + 2, j0 : j0 + n].rearrange("p i n -> p n i"),
+            )
+
+        for i in range(3):
+            for j0 in range(0, S, HALF):
+                gather(i, j0, HALF)
+            if i == 1:
+                interleave(0, 0, S)
+
+        spare = psum.tile([P, 4, P], F32, name="wgt_cols2")
+        for r in range(WARM):
+            nc.tensor.transpose(spare[:, r % 4, :], g[:, 2, (r % 4) * P : (r % 4 + 1) * P], ident[:])
+        for r in range(WARM):
+            nc.tensor.transpose(spare[:, r % 4, :], planes[3][:, r * P : (r + 1) * P], ident[:])
+
+        accs = {}
+
+        def multiply(s):
+            tok = slice(s * TOK, (s + 1) * TOK)
+            nc.vector.quantize_mx(
+                out=xc[:, tok].bitcast(FP8X4), scales=xs[:, tok], in_=xg[:, tok, :].rearrange("p n i -> p (n i)")
+            )
+            acc = psum.tile([TOK, M], F32, name=f"acc{s % 3}")
+            for q in range(2):
+                nc.tensor.matmul_mx(
+                    out=acc[:],
+                    lhsT=xc[:, tok].bitcast(FP8X4),
+                    lhsT_scale=xs[:, tok],
+                    rhs=codes[q][:].bitcast(FP8X4),
+                    rhs_scale=scales[q][:],
+                    start=(q == 0),
+                    stop=(q == 1),
+                )
+            accs[s] = acc
+
+        def finish(s, pieces):
+            tok = slice(s * TOK, (s + 1) * TOK)
+            y = keep.tile([TOK, M], F32, name=f"y{s}")
+            o = keep.tile([TOK, M], F32, name=f"o{s}")
+            width = M // pieces
+            for k in range(pieces):
+                col = slice(k * width, (k + 1) * width)
+                nc.vector.tensor_tensor(y[:, col], accs[s][:, col], b_all[:, col], ALU.add)
+                nc.scalar.activation(o[:, col], y[:, col], ACT.Silu)
+                nc.sync.dma_start(out=out[tok, col], in_=o[:, col])
+
+        def step(s):
+            gather(3, s * TOK, TOK)
+            interleave(2, s * TOK, TOK)
+
+        step(0)
+        step(1)
+        step(2)
+        multiply(0)
+        step(3)
+        multiply(1)
+        finish(0, 1)
+        multiply(2)
+        finish(1, 1)
+        multiply(3)
+        finish(2, 1)
+        finish(3, 2)

@@ -7,7 +7,7 @@ P = 128
 PACK = 4
 TOK = 128
 HALF = 256
-WARM = 12
+WARM = 16
 FLOPS = 2 * 2 * K * M * S
 
 F32 = mybir.dt.float32
@@ -20,7 +20,7 @@ FP8X4 = mybir.dt.float8_e4m3fn_x4
 ALU = mybir.AluOpType
 ACT = mybir.ActivationFunctionType
 
-HI_MASK = -(1 << 20)
+HI_MASK = -0x000F0010
 
 
 def tile_list_heads_tm_hl_silu_kernel(tc, xT, w, wgt, b, offs, out):
@@ -29,22 +29,18 @@ def tile_list_heads_tm_hl_silu_kernel(tc, xT, w, wgt, b, offs, out):
         keep = ctx.enter_context(tc.tile_pool(name="keep", bufs=1))
         psum = ctx.enter_context(tc.psum_pool(name="psum", bufs=1))
 
+        b_rows = keep.tile([P, P], F32, name="b_rows")
+        nc.vector.memset(b_rows[:], 0.0)
+        w_f = keep.tile([P, PACK, M], F32, name="w_f", align_bytes=64)
+        nc.sync.dma_start(out=w_f[:], in_=w.rearrange("(p i) n -> p i n", i=PACK))
         wgt_rows = keep.tile([P, P], F32, name="wgt_rows")
         nc.sync.dma_start(
             out=wgt_rows[:],
             in_=wgt.rearrange("(g r) (c m) -> g r c m", r=16, m=P)[:, 0:4, :, :].rearrange("g a c m -> g (a c) m"),
         )
-        b_rows = keep.tile([P, P], F32, name="b_rows")
-        nc.sync.dma_start(
-            out=b_rows[:], in_=b.rearrange("(c m) -> c m", m=P).unsqueeze(0).to_broadcast([P // 4, 4, P])
-        )
         offsets = keep.tile([P, S // 16], U16, name="offsets")
         nc.sync.dma_start(offsets[:], offs)
-
-        w_f = keep.tile([P, PACK, M], F32, name="w_f", align_bytes=64)
-        w_view = w.rearrange("(p i) n -> p i n", i=PACK)
-        for h in range(2):
-            nc.sync.dma_start(out=w_f[:, 2 * h : 2 * h + 2, :], in_=w_view[:, 2 * h : 2 * h + 2, :])
+        nc.sync.dma_start(out=b_rows[0:PACK, :], in_=b.rearrange("(c p) -> c p", p=P))
         x_view = xT.rearrange("(p i) t -> i p t", i=PACK)
         planes = []
         for i in range(PACK):
@@ -94,25 +90,36 @@ def tile_list_heads_tm_hl_silu_kernel(tc, xT, w, wgt, b, offs, out):
         b_all = keep.tile([P, M], F32, name="b_all")
         nc.scalar.copy(b_all[:], b_allp[:])
 
-        hi_bits = keep.tile([P, PACK, M], I32, name="hi_bits")
-        lo_f = keep.tile([P, PACK, M], F32, name="lo_f")
-        hi_f = hi_bits[:].rearrange("p i n -> p (i n)").bitcast(F32).rearrange("p (i n) -> p i n", i=PACK)
-        w_bits = w_f[:].rearrange("p i n -> p (i n)").bitcast(I32).rearrange("p (i n) -> p i n", i=PACK)
+        w_halves = w_f[:].rearrange("p i n -> p (i n)").bitcast(BF16).rearrange("p (i n e) -> p n i e", i=PACK, e=2)
+        upper = keep.tile([P, M, PACK], BF16, name="upper", align_bytes=64)
+        hi = keep.tile([P, M * 2], I32, name="hi", align_bytes=64)
+        lo = keep.tile([P, M, PACK], BF16, name="lo", align_bytes=64)
+        hi_bf = hi[:].bitcast(BF16)
+        codes = [keep.tile([P, M], U32, name=f"codes{q}", align_bytes=64) for q in range(2)]
+        scales = [keep.tile([P, M], U8, name=f"scales{q}", align_bytes=64) for q in range(2)]
         for h in range(2):
-            r = slice(2 * h, 2 * h + 2)
-            nc.vector.tensor_scalar(hi_bits[:, r, :], w_bits[:, r, :], HI_MASK, None, ALU.bitwise_and)
-            nc.vector.tensor_tensor(lo_f[:, r, :], w_f[:, r, :], hi_f[:, r, :], ALU.subtract)
-        codes, scales = [], []
-        for name, part in (("hi", hi_f), ("lo", lo_f[:])):
-            grouped = keep.tile([P, M, PACK], BF16, name=f"grouped_{name}", align_bytes=64)
-            nc.scalar.copy(grouped[:], part.rearrange("p i n -> p n i"))
-            code = keep.tile([P, M], U32, name=f"codes_{name}", align_bytes=64)
-            scale = keep.tile([P, M], U8, name=f"scales_{name}", align_bytes=64)
-            nc.vector.quantize_mx(
-                out=code[:].bitcast(FP8X4), scales=scale[:], in_=grouped[:].rearrange("p n i -> p (n i)")
+            n = slice(h * HALF, (h + 1) * HALF)
+            nc.scalar.copy(upper[:, n, :], w_halves[:, n, :, 1])
+        for h in range(2):
+            n = slice(h * HALF, (h + 1) * HALF)
+            words = slice(h * HALF * 2, (h + 1) * HALF * 2)
+            nc.vector.tensor_scalar(
+                hi[:, words],
+                upper[:, n, :].rearrange("p n i -> p (n i)").bitcast(I32),
+                HI_MASK,
+                None,
+                ALU.bitwise_and,
             )
-            codes.append(code)
-            scales.append(scale)
+        for h in range(2):
+            n = slice(h * HALF, (h + 1) * HALF)
+            nc.vector.tensor_tensor(
+                lo[:, n, :],
+                w_f[:, :, n].rearrange("p i n -> p n i"),
+                hi_bf[:, h * HALF * PACK : (h + 1) * HALF * PACK].rearrange("p (n i) -> p n i", i=PACK),
+                ALU.subtract,
+            )
+        for q, part in enumerate((hi_bf, lo[:].rearrange("p n i -> p (n i)"))):
+            nc.vector.quantize_mx(out=codes[q][:].bitcast(FP8X4), scales=scales[q][:], in_=part)
 
         g = keep.tile([P, PACK, S], F32, name="g", align_bytes=64)
         xg = keep.tile([P, S, PACK], BF16, name="xg", align_bytes=64)
@@ -142,8 +149,6 @@ def tile_list_heads_tm_hl_silu_kernel(tc, xT, w, wgt, b, offs, out):
         spare = psum.tile([P, 4, P], F32, name="wgt_cols2")
         for r in range(WARM):
             nc.tensor.transpose(spare[:, r % 4, :], g[:, 2, (r % 4) * P : (r % 4 + 1) * P], ident[:])
-        for r in range(WARM):
-            nc.tensor.transpose(spare[:, r % 4, :], planes[3][:, r * P : (r + 1) * P], ident[:])
 
         accs = {}
 

@@ -7,7 +7,7 @@ P = 128
 PACK = 4
 TOK = 128
 HALF = 256
-WARM = 16
+WARM = 24
 FLOPS = 2 * 2 * K * M * S
 
 F32 = mybir.dt.float32
@@ -32,7 +32,10 @@ def tile_list_heads_tm_hl_silu_kernel(tc, xT, w, wgt, b, offs, out):
         b_rows = keep.tile([P, P], F32, name="b_rows")
         nc.vector.memset(b_rows[:], 0.0)
         w_f = keep.tile([P, PACK, M], F32, name="w_f", align_bytes=64)
-        nc.sync.dma_start(out=w_f[:], in_=w.rearrange("(p i) n -> p i n", i=PACK))
+        w_view = w.rearrange("(p i) n -> p i n", i=PACK)
+        for h in range(2):
+            n = slice(h * HALF, (h + 1) * HALF)
+            nc.sync.dma_start(out=w_f[:, :, n], in_=w_view[:, :, n])
         wgt_rows = keep.tile([P, P], F32, name="wgt_rows")
         nc.sync.dma_start(
             out=wgt_rows[:],
@@ -110,14 +113,16 @@ def tile_list_heads_tm_hl_silu_kernel(tc, xT, w, wgt, b, offs, out):
                 None,
                 ALU.bitwise_and,
             )
+        low = keep.tile([P, PACK, M], BF16, name="low", align_bytes=64)
         for h in range(2):
             n = slice(h * HALF, (h + 1) * HALF)
             nc.vector.tensor_tensor(
-                lo[:, n, :],
-                w_f[:, :, n].rearrange("p i n -> p n i"),
-                hi_bf[:, h * HALF * PACK : (h + 1) * HALF * PACK].rearrange("p (n i) -> p n i", i=PACK),
+                low[:, :, n],
+                w_f[:, :, n],
+                hi_bf[:, h * HALF * PACK : (h + 1) * HALF * PACK].rearrange("p (n i) -> p i n", i=PACK),
                 ALU.subtract,
             )
+            nc.scalar.copy(lo[:, n, :], low[:, :, n].rearrange("p i n -> p n i"))
         for q, part in enumerate((hi_bf, lo[:].rearrange("p n i -> p (n i)"))):
             nc.vector.quantize_mx(out=codes[q][:].bitcast(FP8X4), scales=scales[q][:], in_=part)
 
@@ -148,7 +153,7 @@ def tile_list_heads_tm_hl_silu_kernel(tc, xT, w, wgt, b, offs, out):
 
         spare = psum.tile([P, 4, P], F32, name="wgt_cols2")
         for r in range(WARM):
-            nc.tensor.transpose(spare[:, r % 4, :], g[:, 2, (r % 4) * P : (r % 4 + 1) * P], ident[:])
+            nc.tensor.transpose(spare[:, r % 4, :], planes[2][:, (r % 16) * P : (r % 16 + 1) * P], ident[:])
 
         accs = {}
 

from contextlib import ExitStack

import concourse.mybir as mybir

K, M, T, S = 512, 512, 2048, 512
P = 128
PACK = 4
TOK = 128
HALF = 256
WARM = 24
FLOPS = 2 * 2 * K * M * S

F32 = mybir.dt.float32
BF16 = mybir.dt.bfloat16
I32 = mybir.dt.int32
U32 = mybir.dt.uint32
U16 = mybir.dt.uint16
U8 = mybir.dt.uint8
FP8X4 = mybir.dt.float8_e4m3fn_x4
ALU = mybir.AluOpType
ACT = mybir.ActivationFunctionType

HI_MASK = -0x000F0010


def tile_list_heads_tm_hl_silu_kernel(tc, xT, w, wgt, b, offs, out):
    nc = tc.nc
    with ExitStack() as ctx:
        keep = ctx.enter_context(tc.tile_pool(name="keep", bufs=1))
        psum = ctx.enter_context(tc.psum_pool(name="psum", bufs=1))

        b_rows = keep.tile([P, P], F32, name="b_rows")
        nc.vector.memset(b_rows[:], 0.0)
        w_f = keep.tile([P, PACK, M], F32, name="w_f", align_bytes=64)
        w_view = w.rearrange("(p i) n -> p i n", i=PACK)
        for h in range(2):
            n = slice(h * HALF, (h + 1) * HALF)
            nc.sync.dma_start(out=w_f[:, :, n], in_=w_view[:, :, n])
        wgt_rows = keep.tile([P, P], F32, name="wgt_rows")
        nc.sync.dma_start(
            out=wgt_rows[:],
            in_=wgt.rearrange("(g r) (c m) -> g r c m", r=16, m=P)[:, 0:4, :, :].rearrange("g a c m -> g (a c) m"),
        )
        offsets = keep.tile([P, S // 16], U16, name="offsets")
        nc.sync.dma_start(offsets[:], offs)
        nc.sync.dma_start(out=b_rows[0:PACK, :], in_=b.rearrange("(c p) -> c p", p=P))
        x_view = xT.rearrange("(p i) t -> i p t", i=PACK)
        planes = []
        for i in range(PACK):
            plane = keep.tile([P, T], F32, name=f"plane{i}")
            nc.sync.dma_start(out=plane[:], in_=x_view[i])
            planes.append(plane)

        warm = keep.tile([P, 1], F32, name="warm")
        nc.vector.memset(warm[:], 0.0)
        nc.scalar.activation(warm[:], warm[:], ACT.Silu)


        ones = keep.tile([P, P], F32, name="ones")
        nc.vector.memset(ones[:], 1.0)
        col = keep.tile([P, P], F32, name="col", align_bytes=64)
        nc.vector.tensor_tensor_scan(col[:], ones[:], ones[:], 0.0, ALU.mult, ALU.add)
        blocks = keep.tile([P, P], F32, name="blocks")
        nc.vector.memset(blocks[:], 0.0)
        for q in range(4):
            nc.vector.memset(blocks[32 * q : 32 * q + 32, 32 * q : 32 * q + 32], 1.0)
        row = keep.tile([P, P], F32, name="row", align_bytes=64)
        nc.vector.transpose(row[:], col[:])
        same = keep.tile([P, P], F32, name="same")
        nc.vector.tensor_tensor(same[:], col[:], row[:], ALU.is_equal)
        ident = keep.tile([P, P], F32, name="ident")
        nc.vector.tensor_tensor(ident[:], same[:], blocks[:], ALU.mult)

        wgt_cols = psum.tile([P, P], F32, name="wgt_cols")
        nc.tensor.transpose(wgt_cols[:], wgt_rows[:], ident[:])
        b_colp = psum.tile([P, P], F32, name="b_colp")
        nc.tensor.transpose(b_colp[:], b_rows[:], ident[:])
        wgt_rep = keep.tile([P, 4, P], F32, name="wgt_rep")
        nc.scalar.copy(
            wgt_rep[:].rearrange("p c (g r) -> p c g r", r=16),
            wgt_cols[:].rearrange("m (g a c) -> m c g a", g=8, c=4)[:, :, :, 0:1].to_broadcast([P, 4, 8, 16]),
        )
        b_col = keep.tile([P, PACK], F32, name="b_col")
        nc.scalar.copy(b_col[:], b_colp[:, 0:PACK])
        wgt_allp = psum.tile([P, S], F32, name="wgt_allp")
        b_allp = psum.tile([P, M], F32, name="b_allp")
        for c in range(4):
            nc.tensor.transpose(wgt_allp[:, c * P : (c + 1) * P], wgt_rep[:, c, :], ident[:])
        for c in range(PACK):
            nc.tensor.transpose(b_allp[:, c * P : (c + 1) * P], b_col[:, c : c + 1].to_broadcast([P, P]), ident[:])
        wgt_t = keep.tile([P, S], F32, name="wgt_t")
        nc.scalar.copy(wgt_t[:], wgt_allp[:])
        b_all = keep.tile([P, M], F32, name="b_all")
        nc.scalar.copy(b_all[:], b_allp[:])

        w_halves = w_f[:].rearrange("p i n -> p (i n)").bitcast(BF16).rearrange("p (i n e) -> p n i e", i=PACK, e=2)
        upper = keep.tile([P, M, PACK], BF16, name="upper", align_bytes=64)
        hi = keep.tile([P, M * 2], I32, name="hi", align_bytes=64)
        lo = keep.tile([P, M, PACK], BF16, name="lo", align_bytes=64)
        hi_bf = hi[:].bitcast(BF16)
        codes = [keep.tile([P, M], U32, name=f"codes{q}", align_bytes=64) for q in range(2)]
        scales = [keep.tile([P, M], U8, name=f"scales{q}", align_bytes=64) for q in range(2)]
        for h in range(2):
            n = slice(h * HALF, (h + 1) * HALF)
            nc.scalar.copy(upper[:, n, :], w_halves[:, n, :, 1])
        for h in range(2):
            n = slice(h * HALF, (h + 1) * HALF)
            words = slice(h * HALF * 2, (h + 1) * HALF * 2)
            nc.vector.tensor_scalar(
                hi[:, words],
                upper[:, n, :].rearrange("p n i -> p (n i)").bitcast(I32),
                HI_MASK,
                None,
                ALU.bitwise_and,
            )
        low = keep.tile([P, PACK, M], BF16, name="low", align_bytes=64)
        for h in range(2):
            n = slice(h * HALF, (h + 1) * HALF)
            nc.vector.tensor_tensor(
                low[:, :, n],
                w_f[:, :, n],
                hi_bf[:, h * HALF * PACK : (h + 1) * HALF * PACK].rearrange("p (n i) -> p i n", i=PACK),
                ALU.subtract,
            )
            nc.scalar.copy(lo[:, n, :], low[:, :, n].rearrange("p i n -> p n i"))
        for q, part in enumerate((hi_bf, lo[:].rearrange("p n i -> p (n i)"))):
            nc.vector.quantize_mx(out=codes[q][:].bitcast(FP8X4), scales=scales[q][:], in_=part)

        g = keep.tile([P, PACK, S], F32, name="g", align_bytes=64)
        xg = keep.tile([P, S, PACK], BF16, name="xg", align_bytes=64)
        xc = keep.tile([P, S], U32, name="xc", align_bytes=64)
        xs = keep.tile([P, S], U8, name="xs", align_bytes=64)

        def gather(i, j0, n):
            nc.vector.tensor_tensor(
                g[:, i, j0 : j0 + n],
                planes[i][:].indirect(offsets[:, j0 // 16 : (j0 + n) // 16]),
                wgt_t[:, j0 : j0 + n],
                ALU.mult,
            )

        def interleave(i0, j0, n):
            nc.scalar.copy(
                xg[:, j0 : j0 + n, i0 : i0 + 2],
                g[:, i0 : i0 + 2, j0 : j0 + n].rearrange("p i n -> p n i"),
            )

        for i in range(3):
            for j0 in range(0, S, HALF):
                gather(i, j0, HALF)
            if i == 1:
                interleave(0, 0, S)

        spare = psum.tile([P, 4, P], F32, name="wgt_cols2")
        for r in range(WARM):
            nc.tensor.transpose(spare[:, r % 4, :], planes[2][:, (r % 16) * P : (r % 16 + 1) * P], ident[:])

        accs = {}

        def multiply(s):
            tok = slice(s * TOK, (s + 1) * TOK)
            nc.vector.quantize_mx(
                out=xc[:, tok].bitcast(FP8X4), scales=xs[:, tok], in_=xg[:, tok, :].rearrange("p n i -> p (n i)")
            )
            acc = psum.tile([TOK, M], F32, name=f"acc{s % 3}")
            for q in range(2):
                nc.tensor.matmul_mx(
                    out=acc[:],
                    lhsT=xc[:, tok].bitcast(FP8X4),
                    lhsT_scale=xs[:, tok],
                    rhs=codes[q][:].bitcast(FP8X4),
                    rhs_scale=scales[q][:],
                    start=(q == 0),
                    stop=(q == 1),
                )
            accs[s] = acc

        def finish(s, pieces):
            tok = slice(s * TOK, (s + 1) * TOK)
            y = keep.tile([TOK, M], F32, name=f"y{s}")
            o = keep.tile([TOK, M], F32, name=f"o{s}")
            width = M // pieces
            for k in range(pieces):
                col = slice(k * width, (k + 1) * width)
                nc.vector.tensor_tensor(y[:, col], accs[s][:, col], b_all[:, col], ALU.add)
                nc.scalar.activation(o[:, col], y[:, col], ACT.Silu)
                nc.sync.dma_start(out=out[tok, col], in_=o[:, col])

        def step(s):
            gather(3, s * TOK, TOK)
            interleave(2, s * TOK, TOK)

        step(0)
        step(1)
        step(2)
        multiply(0)
        step(3)
        multiply(1)
        finish(0, 1)
        multiply(2)
        finish(1, 1)
        multiply(3)
        finish(2, 1)
        finish(3, 2)
